import numpy as np
import ml_dtypes


def mxq(x, axis, fmt="e4m3"):
    dtype, down = {"e4m3": (ml_dtypes.float8_e4m3fn, 7), "e5m2": (ml_dtypes.float8_e5m2, 14)}[fmt]
    v = np.moveaxis(np.asarray(x, np.float32).astype(ml_dtypes.bfloat16).astype(np.float64), axis, -1)
    blocks = v.reshape(v.shape[:-1] + (-1, 32))
    amax = np.abs(blocks).max(-1, keepdims=True)
    byte = np.maximum(np.where(amax > 0, np.frexp(amax)[1] - 1 + 127, 0) - down, 1)
    scale = np.exp2(byte - 127.0)
    codes = (blocks / scale).astype(np.float32).astype(dtype).astype(np.float64)
    return np.moveaxis((codes * scale).reshape(v.shape), -1, axis)


WIDE = False


def mx_kscale(k, group=512):
    if not WIDE:
        return np.ones(k)
    levels = np.array([18, -18])
    if group != 512:
        return np.exp2(np.random.permutation(np.resize(levels, k // group))).repeat(group)
    if k % 512:
        return np.exp2(np.random.permutation(np.resize(levels, k // 32))).repeat(32)
    a = np.empty((k // 512, 16))
    for p in range(k // 512):
        a[p, :8] = np.random.permutation(np.resize(levels, 8))
        for g in range(8):
            far = levels[np.abs(levels - a[p, g]) >= 10]
            a[p, g + 8] = far[np.random.randint(len(far))]
    return np.exp2(a.ravel()).repeat(32)


def f64(x):
    return np.asarray(x).astype(np.float64)


G, D, M, N = 4, 128, 256, 1024


def setup_inputs():
    n = np.random.standard_normal
    s = mx_kscale(D, 0)[:, None]
    return {
        "x": (n((G, D, N)) * s).astype(np.float32),
        "w": (n((G, D, M)) / np.sqrt(D) / s).astype(np.float32),
    }


def reference(x, w):
    xq = mxq(f64(x), 1, "e4m3")
    y = mxq(f64(w), 1, "e4m3").transpose(0, 2, 1) @ xq
    y = np.tanh(y)
    return y

@@ -1,0 +1,125 @@
+from contextlib import ExitStack
+
+import concourse.mybir as mybir
+
+G, D, M, N = 4, 128, 256, 1024
+FLOPS = 2 * G * D * M * N
+
+F32 = mybir.dt.float32
+BF16 = mybir.dt.bfloat16
+U32 = mybir.dt.uint32
+U8 = mybir.dt.uint8
+FP8X4 = mybir.dt.float8_e4m3fn_x4
+TANH = mybir.ActivationFunctionType.Tanh
+
+P = 128
+PACK = 4
+ROWS = 32
+U = 128
+
+LOADS = [["x",0,128,"sync"],["w",0,128,"sync"],["w",128,256,"sync"],["x",128,256,"sync"],["x",256,512,"sync"],["x",512,1024,"sync"]]
+VEC = [["c","x",0,128],["q","x",0,128],["c","w",0,128],["q","w",0,128],["c","w",128,256],["c","x",128,256],["q","w",128,256],["q","x",128,256],["c","x",256,384],["c","x",384,512],["q","x",256,384],["q","x",384,512],["c","x",512,768],["q","x",512,768],["c","x",768,1024],["q","x",768,1024]]
+ACTS = [[[0,[0],0,128]],[[1,[0],0,128]],[[2,[0],0,128]],[[3,[0],0,128]],[[0,[1],0,128]],[[1,[1],0,128]],[[2,[1],0,128]],[[3,[1],0,128]],[[0,[0,1],128,256]],[[1,[0,1],128,256]],[[2,[0,1],128,256]],[[3,[0,1],128,256]],[[0,[0,1],256,512]],[[1,[0,1],256,512]],[[2,[0,1],256,512]],[[3,[0,1],256,512]],[[0,[0,1],512,768]],[[1,[0,1],512,768]],[[2,[0,1],512,768]],[[0,[0,1],768,1024]],[[1,[0,1],768,1024]],[[2,[0,1],768,1024]],[[3,[0],512,1024]],[[3,[1],512,1024]]]
+STORES = [[0,4,0,256,"sync"],[4,8,0,256,"sync"],[0,4,256,512,"sync"],[4,8,256,512,"sync"],[0,2,512,1024,"sync"],[2,4,512,1024,"sync"],[4,6,512,1024,"sync"],[6,8,512,1024,"sync"]]
+WARM = True
+BLOCK4 = False
+
+
+def tile_rows_glin_tanh_kernel(tc, x, w, out):
+    nc = tc.nc
+    src = {
+        "x": x.rearrange("g (p j) n -> (g p) j n", j=PACK),
+        "w": w.rearrange("g (p j) m -> (g p) j m", j=PACK),
+    }
+    dst = out.rearrange("g (h s) n -> s (g h) n", s=P)
+    queue = {"sync": nc.sync, "scalar": nc.scalar, "gpsimd": nc.gpsimd}
+
+    with ExitStack() as ctx:
+        sb = ctx.enter_context(tc.tile_pool(name="sb", bufs=1))
+        ps = ctx.enter_context(tc.psum_pool(name="ps", bufs=1))
+        ctx.enter_context(tc.manual_schedule())
+
+        raw = []
+        for i, (name, c0, c1, q) in enumerate(LOADS):
+            t = sb.tile([P, PACK, c1 - c0], F32, name="raw%d" % i, align_bytes=64)
+            queue[q].dma_start(out=t[:], in_=src[name][:, :, c0:c1])
+            raw.append((name, c0, c1, t))
+
+        if WARM:
+            warm_in = sb.tile([P, 8], F32, name="warm_in")
+            warm_out = sb.tile([P, 8], F32, name="warm_out")
+            nc.gpsimd.memset(warm_in[:], 0.0)
+            nc.scalar.activation(out=warm_out[:, 0:1], in_=warm_in[:, 0:1], func=TANH)
+
+        grouped = {}
+        coded = []
+        for op, name, c0, c1 in VEC:
+            if op != "q":
+                t = sb.tile([P, c1 - c0, PACK], BF16, name="grp_%s%d" % (name, c0), align_bytes=64)
+                rname, r0, r1, r = [e for e in raw if e[0] == name and e[1] <= c0 and c1 <= e[2]][0]
+                piece = r[:, :, c0 - r0 : c1 - r0]
+                if BLOCK4:
+                    o = t[:].rearrange("p (c i) j -> p c j i", i=4)
+                    s = piece.rearrange("p j (c i) -> p c j i", i=4)
+                else:
+                    o = t[:]
+                    s = piece.rearrange("p j c -> p c j")
+                if op == "c":
+                    nc.vector.tensor_copy(out=o, in_=s)
+                else:
+                    nc.scalar.copy(out=o, in_=s)
+                grouped[(name, c0)] = t
+            else:
+                codes = sb.tile([P, c1 - c0], U32, name="codes_%s%d" % (name, c0), align_bytes=64)
+                scales = sb.tile([P, c1 - c0], U8, name="scales_%s%d" % (name, c0), align_bytes=64)
+                nc.vector.quantize_mx(
+                    out=codes[:].bitcast(FP8X4),
+                    scales=scales[:],
+                    in_=grouped[(name, c0)][:].rearrange("p c j -> p (c j)"),
+                )
+                coded.append((name, c0, c1, codes, scales))
+
+        def operand(name, g, c0, width):
+            cname, q0, q1, codes, scales = [e for e in coded if e[0] == name and e[1] <= c0 and c0 + width <= e[2]][0]
+            rows = slice(ROWS * g, ROWS * (g + 1))
+            cols = slice(c0 - q0, c0 - q0 + width)
+            return codes[rows, cols].bitcast(FP8X4), scales[rows, cols]
+
+        banks = [[ps.tile([P, 512], F32, name="bank%d_%d" % (g, b)) for b in range(2)] for g in range(G)]
+        res = [sb.tile([P, k1 - k0, c1 - c0], F32, name="res%d" % i) for i, (k0, k1, c0, c1, q) in enumerate(STORES)]
+        left = [(k1 - k0) * (c1 - c0) for (k0, k1, c0, c1, q) in STORES]
+        used = [0] * G
+
+        for wave in ACTS:
+            calls = []
+            mine = []
+            for g, halves, c0, c1 in wave:
+                bank = banks[g][used[g] % 2]
+                used[g] += 1
+                mine.append(bank)
+                calls.append([(g, bank, i, h, c, c0, c1) for i, h in enumerate(halves) for c in range(c0, c1, U)])
+            for r in range(max(len(c) for c in calls)):
+                for cl in calls:
+                    if r < len(cl):
+                        g, bank, i, h, c, c0, c1 = cl[r]
+                        lhs, lhs_s = operand("w", g, P * h, P)
+                        rhs, rhs_s = operand("x", g, c, U)
+                        at = i * (c1 - c0) + c - c0
+                        nc.tensor.matmul_mx(
+                            out=bank[:, at : at + U], lhsT=lhs, lhsT_scale=lhs_s, rhs=rhs, rhs_scale=rhs_s,
+                            start=True, stop=True,
+                        )
+            for (g, halves, c0, c1), bank in zip(wave, mine):
+                k0 = 2 * g + halves[0]
+                k1 = 2 * g + halves[-1] + 1
+                i = [j for j, e in enumerate(STORES) if e[0] <= k0 and k1 <= e[1] and e[2] <= c0 and c1 <= e[3]][0]
+                s0, s1, t0, t1, q = STORES[i]
+                width = c1 - c0
+                nc.scalar.activation(
+                    out=res[i][:, k0 - s0 : k1 - s0, c0 - t0 : c1 - t0],
+                    in_=bank[:, 0 : len(halves) * width].rearrange("p (h c) -> p h c", c=width),
+                    func=TANH,
+                )
+                left[i] -= len(halves) * width
+                if left[i] == 0:
+                    queue[q].dma_start(out=dst[:, s0:s1, t0:t1], in_=res[i][:])

@@ -17,10 +17,10 @@ PACK = 4
 ROWS = 32
 U = 128
 
-LOADS = [["x",0,128,"sync"],["w",0,128,"sync"],["w",128,256,"sync"],["x",128,256,"sync"],["x",256,512,"sync"],["x",512,1024,"sync"]]
-VEC = [["c","x",0,128],["q","x",0,128],["c","w",0,128],["q","w",0,128],["c","w",128,256],["c","x",128,256],["q","w",128,256],["q","x",128,256],["c","x",256,384],["c","x",384,512],["q","x",256,384],["q","x",384,512],["c","x",512,768],["q","x",512,768],["c","x",768,1024],["q","x",768,1024]]
-ACTS = [[[0,[0],0,128]],[[1,[0],0,128]],[[2,[0],0,128]],[[3,[0],0,128]],[[0,[1],0,128]],[[1,[1],0,128]],[[2,[1],0,128]],[[3,[1],0,128]],[[0,[0,1],128,256]],[[1,[0,1],128,256]],[[2,[0,1],128,256]],[[3,[0,1],128,256]],[[0,[0,1],256,512]],[[1,[0,1],256,512]],[[2,[0,1],256,512]],[[3,[0,1],256,512]],[[0,[0,1],512,768]],[[1,[0,1],512,768]],[[2,[0,1],512,768]],[[0,[0,1],768,1024]],[[1,[0,1],768,1024]],[[2,[0,1],768,1024]],[[3,[0],512,1024]],[[3,[1],512,1024]]]
-STORES = [[0,4,0,256,"sync"],[4,8,0,256,"sync"],[0,4,256,512,"sync"],[4,8,256,512,"sync"],[0,2,512,1024,"sync"],[2,4,512,1024,"sync"],[4,6,512,1024,"sync"],[6,8,512,1024,"sync"]]
+LOADS = [["w",0,256,"sync"],["x",0,256,"sync"],["x",256,512,"sync"],["x",512,1024,"sync"]]
+VEC = [["c","w",0,128],["c","w",128,256],["q","w",0,128],["q","w",128,256],["c","x",0,128],["c","x",128,256],["q","x",0,128],["q","x",128,256],["c","x",256,384],["c","x",384,512],["q","x",256,384],["q","x",384,512],["c","x",512,768],["q","x",512,768],["c","x",768,1024],["q","x",768,1024]]
+ACTS = [[[0,[0,1],0,256]],[[1,[0,1],0,256]],[[2,[0,1],0,256]],[[2,[0,1],256,512]],[[3,[0,1],0,256]],[[3,[0,1],256,512]],[[0,[0,1],256,512]],[[1,[0,1],256,512]],[[0,[0,1],512,768]],[[1,[0,1],512,768]],[[0,[0,1],768,1024]],[[1,[0,1],768,1024]],[[2,[0],512,1024]],[[2,[1],512,1024]],[[3,[0],512,1024]],[[3,[1],512,1024]]]
+STORES = [[0,2,0,256,"sync"],[2,4,0,256,"sync"],[4,6,0,512,"sync"],[6,8,0,512,"sync"],[0,4,256,512,"sync"],[0,2,512,1024,"sync"],[2,4,512,1024,"sync"],[4,6,512,1024,"sync"],[6,8,512,1024,"sync"]]
 WARM = True
 BLOCK4 = False
 

@@ -19,8 +19,8 @@ U = 128
 
 LOADS = [["w",0,256,"sync"],["x",0,256,"sync"],["x",256,512,"sync"],["x",512,1024,"sync"]]
 VEC = [["c","w",0,128],["c","w",128,256],["q","w",0,128],["q","w",128,256],["c","x",0,128],["c","x",128,256],["q","x",0,128],["q","x",128,256],["c","x",256,384],["c","x",384,512],["q","x",256,384],["q","x",384,512],["c","x",512,768],["q","x",512,768],["c","x",768,1024],["q","x",768,1024]]
-ACTS = [[[0,[0,1],0,256]],[[1,[0,1],0,256]],[[2,[0,1],0,256]],[[2,[0,1],256,512]],[[3,[0,1],0,256]],[[3,[0,1],256,512]],[[0,[0,1],256,512]],[[1,[0,1],256,512]],[[0,[0,1],512,768]],[[1,[0,1],512,768]],[[0,[0,1],768,1024]],[[1,[0,1],768,1024]],[[2,[0],512,1024]],[[2,[1],512,1024]],[[3,[0],512,1024]],[[3,[1],512,1024]]]
-STORES = [[0,2,0,256,"sync"],[2,4,0,256,"sync"],[4,6,0,512,"sync"],[6,8,0,512,"sync"],[0,4,256,512,"sync"],[0,2,512,1024,"sync"],[2,4,512,1024,"sync"],[4,6,512,1024,"sync"],[6,8,512,1024,"sync"]]
+ACTS = [["mm",[[0,0,[0,1],0,256],[1,0,[0,1],0,256],[2,0,[0,1],0,256],[3,0,[0,1],0,256]]],["mm",[[2,1,[0,1],256,512],[3,1,[0,1],256,512],[0,1,[0,1],256,512],[1,1,[0,1],256,512]]],["act",[[0,0,[0,1],0,256],[1,0,[0,1],0,256],[2,0,[0,1],0,256],[2,1,[0,1],256,512],[3,0,[0,1],0,256],[3,1,[0,1],256,512]]],["mm",[[0,0,[0,1],512,768],[1,0,[0,1],512,768]]],["act",[[0,1,[0,1],256,512],[1,1,[0,1],256,512]]],["mm",[[0,1,[0,1],768,1024],[1,1,[0,1],768,1024],[2,0,[0],512,1024],[3,0,[0],512,1024]]],["mm",[[2,1,[1],512,1024],[3,1,[1],512,1024]]],["act",[[0,0,[0,1],512,768],[1,0,[0,1],512,768],[0,1,[0,1],768,1024],[1,1,[0,1],768,1024],[2,0,[0],512,1024],[2,1,[1],512,1024],[3,0,[0],512,1024],[3,1,[1],512,1024]]]]
+STORES = [[0,2,0,256,"sync"],[2,4,0,256,"sync"],[4,6,0,512,"sync"],[6,8,0,512,"sync"],[0,4,256,512,"sync"],[0,2,512,1024,"sync"],[2,4,512,1024,"sync"],[4,6,512,1024,"sync"],[6,7,512,1024,"sync"],[7,8,512,1024,"sync"]]
 WARM = True
 BLOCK4 = False
 
@@ -88,38 +88,35 @@ def tile_rows_glin_tanh_kernel(tc, x, w, out):
         banks = [[ps.tile([P, 512], F32, name="bank%d_%d" % (g, b)) for b in range(2)] for g in range(G)]
         res = [sb.tile([P, k1 - k0, c1 - c0], F32, name="res%d" % i) for i, (k0, k1, c0, c1, q) in enumerate(STORES)]
         left = [(k1 - k0) * (c1 - c0) for (k0, k1, c0, c1, q) in STORES]
-        used = [0] * G
-
-        for wave in ACTS:
-            calls = []
-            mine = []
-            for g, halves, c0, c1 in wave:
-                bank = banks[g][used[g] % 2]
-                used[g] += 1
-                mine.append(bank)
-                calls.append([(g, bank, i, h, c, c0, c1) for i, h in enumerate(halves) for c in range(c0, c1, U)])
-            for r in range(max(len(c) for c in calls)):
-                for cl in calls:
-                    if r < len(cl):
-                        g, bank, i, h, c, c0, c1 = cl[r]
-                        lhs, lhs_s = operand("w", g, P * h, P)
-                        rhs, rhs_s = operand("x", g, c, U)
-                        at = i * (c1 - c0) + c - c0
-                        nc.tensor.matmul_mx(
-                            out=bank[:, at : at + U], lhsT=lhs, lhsT_scale=lhs_s, rhs=rhs, rhs_scale=rhs_s,
-                            start=True, stop=True,
-                        )
-            for (g, halves, c0, c1), bank in zip(wave, mine):
-                k0 = 2 * g + halves[0]
-                k1 = 2 * g + halves[-1] + 1
-                i = [j for j, e in enumerate(STORES) if e[0] <= k0 and k1 <= e[1] and e[2] <= c0 and c1 <= e[3]][0]
-                s0, s1, t0, t1, q = STORES[i]
-                width = c1 - c0
-                nc.scalar.activation(
-                    out=res[i][:, k0 - s0 : k1 - s0, c0 - t0 : c1 - t0],
-                    in_=bank[:, 0 : len(halves) * width].rearrange("p (h c) -> p h c", c=width),
-                    func=TANH,
-                )
-                left[i] -= len(halves) * width
-                if left[i] == 0:
-                    queue[q].dma_start(out=dst[:, s0:s1, t0:t1], in_=res[i][:])
+        for kind, items in ACTS:
+            if kind == "mm":
+                calls = [
+                    [(g, banks[g][b], i, h, c, c0, c1) for c in range(c0, c1, U) for i, h in enumerate(halves)]
+                    for g, b, halves, c0, c1 in items
+                ]
+                for r in range(max(len(c) for c in calls)):
+                    for cl in calls:
+                        if r < len(cl):
+                            g, bank, i, h, c, c0, c1 = cl[r]
+                            lhs, lhs_s = operand("w", g, P * h, P)
+                            rhs, rhs_s = operand("x", g, c, U)
+                            at = i * (c1 - c0) + c - c0
+                            nc.tensor.matmul_mx(
+                                out=bank[:, at : at + U], lhsT=lhs, lhsT_scale=lhs_s, rhs=rhs, rhs_scale=rhs_s,
+                                start=True, stop=True,
+                            )
+            else:
+                for g, b, halves, c0, c1 in items:
+                    k0 = 2 * g + halves[0]
+                    k1 = 2 * g + halves[-1] + 1
+                    i = [j for j, e in enumerate(STORES) if e[0] <= k0 and k1 <= e[1] and e[2] <= c0 and c1 <= e[3]][0]
+                    s0, s1, t0, t1, q = STORES[i]
+                    width = c1 - c0
+                    nc.scalar.activation(
+                        out=res[i][:, k0 - s0 : k1 - s0, c0 - t0 : c1 - t0],
+                        in_=banks[g][b][:, 0 : len(halves) * width].rearrange("p (h c) -> p h c", c=width),
+                        func=TANH,
+                    )
+                    left[i] -= len(halves) * width
+                    if left[i] == 0:
+                        queue[q].dma_start(out=dst[:, s0:s1, t0:t1], in_=res[i][:])

@@ -18,11 +18,11 @@ ROWS = 32
 U = 128
 
 LOADS = [["w",0,256,"sync"],["x",0,256,"sync"],["x",256,512,"sync"],["x",512,1024,"sync"]]
-VEC = [["c","w",0,128],["c","w",128,256],["q","w",0,128],["q","w",128,256],["c","x",0,128],["c","x",128,256],["q","x",0,128],["q","x",128,256],["c","x",256,384],["c","x",384,512],["q","x",256,384],["q","x",384,512],["c","x",512,768],["q","x",512,768],["c","x",768,1024],["q","x",768,1024]]
+VEC = [["c","w",0,128],["s","w",128,256],["q","w",0,128],["q","w",128,256],["c","x",0,128],["s","x",128,256],["q","x",0,128],["q","x",128,256],["c","x",256,384],["c","x",384,512],["q","x",256,384],["q","x",384,512],["c","x",512,768],["q","x",512,768],["c","x",768,1024],["q","x",768,1024]]
 ACTS = [["mm",[[0,0,[0,1],0,256],[1,0,[0,1],0,256],[2,0,[0,1],0,256],[3,0,[0,1],0,256]]],["mm",[[2,1,[0,1],256,512],[3,1,[0,1],256,512],[0,1,[0,1],256,512],[1,1,[0,1],256,512]]],["act",[[0,0,[0,1],0,256],[1,0,[0,1],0,256],[2,0,[0,1],0,256],[2,1,[0,1],256,512],[3,0,[0,1],0,256],[3,1,[0,1],256,512]]],["mm",[[0,0,[0,1],512,768],[1,0,[0,1],512,768]]],["act",[[0,1,[0,1],256,512],[1,1,[0,1],256,512]]],["mm",[[0,1,[0,1],768,1024],[1,1,[0,1],768,1024],[2,0,[0],512,1024],[3,0,[0],512,1024]]],["mm",[[2,1,[1],512,1024],[3,1,[1],512,1024]]],["act",[[0,0,[0,1],512,768],[1,0,[0,1],512,768],[0,1,[0,1],768,1024],[1,1,[0,1],768,1024],[2,0,[0],512,1024],[2,1,[1],512,1024],[3,0,[0],512,1024],[3,1,[1],512,1024]]]]
 STORES = [[0,2,0,256,"sync"],[2,4,0,256,"sync"],[4,6,0,512,"sync"],[6,8,0,512,"sync"],[0,4,256,512,"sync"],[0,2,512,1024,"sync"],[2,4,512,1024,"sync"],[4,6,512,1024,"sync"],[6,7,512,1024,"sync"],[7,8,512,1024,"sync"]]
 WARM = True
-BLOCK4 = False
+BLOCK4 = True
 
 
 def tile_rows_glin_tanh_kernel(tc, x, w, out):
@@ -59,8 +59,8 @@ def tile_rows_glin_tanh_kernel(tc, x, w, out):
                 rname, r0, r1, r = [e for e in raw if e[0] == name and e[1] <= c0 and c1 <= e[2]][0]
                 piece = r[:, :, c0 - r0 : c1 - r0]
                 if BLOCK4:
-                    o = t[:].rearrange("p (c i) j -> p c j i", i=4)
-                    s = piece.rearrange("p j (c i) -> p c j i", i=4)
+                    o = t[:].rearrange("p (c i) j -> p c j i", i=2)
+                    s = piece.rearrange("p j (c i) -> p c j i", i=2)
                 else:
                     o = t[:]
                     s = piece.rearrange("p j c -> p c j")

@@ -21,7 +21,7 @@ LOADS = [["w",0,256,"sync"],["x",0,256,"sync"],["x",256,512,"sync"],["x",512,102
 VEC = [["c","w",0,128],["s","w",128,256],["q","w",0,128],["q","w",128,256],["c","x",0,128],["s","x",128,256],["q","x",0,128],["q","x",128,256],["c","x",256,384],["c","x",384,512],["q","x",256,384],["q","x",384,512],["c","x",512,768],["q","x",512,768],["c","x",768,1024],["q","x",768,1024]]
 ACTS = [["mm",[[0,0,[0,1],0,256],[1,0,[0,1],0,256],[2,0,[0,1],0,256],[3,0,[0,1],0,256]]],["mm",[[2,1,[0,1],256,512],[3,1,[0,1],256,512],[0,1,[0,1],256,512],[1,1,[0,1],256,512]]],["act",[[0,0,[0,1],0,256],[1,0,[0,1],0,256],[2,0,[0,1],0,256],[2,1,[0,1],256,512],[3,0,[0,1],0,256],[3,1,[0,1],256,512]]],["mm",[[0,0,[0,1],512,768],[1,0,[0,1],512,768]]],["act",[[0,1,[0,1],256,512],[1,1,[0,1],256,512]]],["mm",[[0,1,[0,1],768,1024],[1,1,[0,1],768,1024],[2,0,[0],512,1024],[3,0,[0],512,1024]]],["mm",[[2,1,[1],512,1024],[3,1,[1],512,1024]]],["act",[[0,0,[0,1],512,768],[1,0,[0,1],512,768],[0,1,[0,1],768,1024],[1,1,[0,1],768,1024],[2,0,[0],512,1024],[2,1,[1],512,1024],[3,0,[0],512,1024],[3,1,[1],512,1024]]]]
 STORES = [[0,2,0,256,"sync"],[2,4,0,256,"sync"],[4,6,0,512,"sync"],[6,8,0,512,"sync"],[0,4,256,512,"sync"],[0,2,512,1024,"sync"],[2,4,512,1024,"sync"],[4,6,512,1024,"sync"],[6,7,512,1024,"sync"],[7,8,512,1024,"sync"]]
-WARM = True
+WARM = False
 BLOCK4 = True
 
 

from contextlib import ExitStack

import concourse.mybir as mybir

G, D, M, N = 4, 128, 256, 1024
FLOPS = 2 * G * D * M * N

F32 = mybir.dt.float32
BF16 = mybir.dt.bfloat16
U32 = mybir.dt.uint32
U8 = mybir.dt.uint8
FP8X4 = mybir.dt.float8_e4m3fn_x4
TANH = mybir.ActivationFunctionType.Tanh

P = 128
PACK = 4
ROWS = 32
U = 128

LOADS = [["w",0,256,"sync"],["x",0,256,"sync"],["x",256,512,"sync"],["x",512,1024,"sync"]]
VEC = [["c","w",0,128],["s","w",128,256],["q","w",0,128],["q","w",128,256],["c","x",0,128],["s","x",128,256],["q","x",0,128],["q","x",128,256],["c","x",256,384],["c","x",384,512],["q","x",256,384],["q","x",384,512],["c","x",512,768],["q","x",512,768],["c","x",768,1024],["q","x",768,1024]]
ACTS = [["mm",[[0,0,[0,1],0,256],[1,0,[0,1],0,256],[2,0,[0,1],0,256],[3,0,[0,1],0,256]]],["mm",[[2,1,[0,1],256,512],[3,1,[0,1],256,512],[0,1,[0,1],256,512],[1,1,[0,1],256,512]]],["act",[[0,0,[0,1],0,256],[1,0,[0,1],0,256],[2,0,[0,1],0,256],[2,1,[0,1],256,512],[3,0,[0,1],0,256],[3,1,[0,1],256,512]]],["mm",[[0,0,[0,1],512,768],[1,0,[0,1],512,768]]],["act",[[0,1,[0,1],256,512],[1,1,[0,1],256,512]]],["mm",[[0,1,[0,1],768,1024],[1,1,[0,1],768,1024],[2,0,[0],512,1024],[3,0,[0],512,1024]]],["mm",[[2,1,[1],512,1024],[3,1,[1],512,1024]]],["act",[[0,0,[0,1],512,768],[1,0,[0,1],512,768],[0,1,[0,1],768,1024],[1,1,[0,1],768,1024],[2,0,[0],512,1024],[2,1,[1],512,1024],[3,0,[0],512,1024],[3,1,[1],512,1024]]]]
STORES = [[0,2,0,256,"sync"],[2,4,0,256,"sync"],[4,6,0,512,"sync"],[6,8,0,512,"sync"],[0,4,256,512,"sync"],[0,2,512,1024,"sync"],[2,4,512,1024,"sync"],[4,6,512,1024,"sync"],[6,7,512,1024,"sync"],[7,8,512,1024,"sync"]]
WARM = False
BLOCK4 = True


def tile_rows_glin_tanh_kernel(tc, x, w, out):
    nc = tc.nc
    src = {
        "x": x.rearrange("g (p j) n -> (g p) j n", j=PACK),
        "w": w.rearrange("g (p j) m -> (g p) j m", j=PACK),
    }
    dst = out.rearrange("g (h s) n -> s (g h) n", s=P)
    queue = {"sync": nc.sync, "scalar": nc.scalar, "gpsimd": nc.gpsimd}

    with ExitStack() as ctx:
        sb = ctx.enter_context(tc.tile_pool(name="sb", bufs=1))
        ps = ctx.enter_context(tc.psum_pool(name="ps", bufs=1))
        ctx.enter_context(tc.manual_schedule())

        raw = []
        for i, (name, c0, c1, q) in enumerate(LOADS):
            t = sb.tile([P, PACK, c1 - c0], F32, name="raw%d" % i, align_bytes=64)
            queue[q].dma_start(out=t[:], in_=src[name][:, :, c0:c1])
            raw.append((name, c0, c1, t))

        if WARM:
            warm_in = sb.tile([P, 8], F32, name="warm_in")
            warm_out = sb.tile([P, 8], F32, name="warm_out")
            nc.gpsimd.memset(warm_in[:], 0.0)
            nc.scalar.activation(out=warm_out[:, 0:1], in_=warm_in[:, 0:1], func=TANH)

        grouped = {}
        coded = []
        for op, name, c0, c1 in VEC:
            if op != "q":
                t = sb.tile([P, c1 - c0, PACK], BF16, name="grp_%s%d" % (name, c0), align_bytes=64)
                rname, r0, r1, r = [e for e in raw if e[0] == name and e[1] <= c0 and c1 <= e[2]][0]
                piece = r[:, :, c0 - r0 : c1 - r0]
                if BLOCK4:
                    o = t[:].rearrange("p (c i) j -> p c j i", i=2)
                    s = piece.rearrange("p j (c i) -> p c j i", i=2)
                else:
                    o = t[:]
                    s = piece.rearrange("p j c -> p c j")
                if op == "c":
                    nc.vector.tensor_copy(out=o, in_=s)
                else:
                    nc.scalar.copy(out=o, in_=s)
                grouped[(name, c0)] = t
            else:
                codes = sb.tile([P, c1 - c0], U32, name="codes_%s%d" % (name, c0), align_bytes=64)
                scales = sb.tile([P, c1 - c0], U8, name="scales_%s%d" % (name, c0), align_bytes=64)
                nc.vector.quantize_mx(
                    out=codes[:].bitcast(FP8X4),
                    scales=scales[:],
                    in_=grouped[(name, c0)][:].rearrange("p c j -> p (c j)"),
                )
                coded.append((name, c0, c1, codes, scales))

        def operand(name, g, c0, width):
            cname, q0, q1, codes, scales = [e for e in coded if e[0] == name and e[1] <= c0 and c0 + width <= e[2]][0]
            rows = slice(ROWS * g, ROWS * (g + 1))
            cols = slice(c0 - q0, c0 - q0 + width)
            return codes[rows, cols].bitcast(FP8X4), scales[rows, cols]

        banks = [[ps.tile([P, 512], F32, name="bank%d_%d" % (g, b)) for b in range(2)] for g in range(G)]
        res = [sb.tile([P, k1 - k0, c1 - c0], F32, name="res%d" % i) for i, (k0, k1, c0, c1, q) in enumerate(STORES)]
        left = [(k1 - k0) * (c1 - c0) for (k0, k1, c0, c1, q) in STORES]
        for kind, items in ACTS:
            if kind == "mm":
                calls = [
                    [(g, banks[g][b], i, h, c, c0, c1) for c in range(c0, c1, U) for i, h in enumerate(halves)]
                    for g, b, halves, c0, c1 in items
                ]
                for r in range(max(len(c) for c in calls)):
                    for cl in calls:
                        if r < len(cl):
                            g, bank, i, h, c, c0, c1 = cl[r]
                            lhs, lhs_s = operand("w", g, P * h, P)
                            rhs, rhs_s = operand("x", g, c, U)
                            at = i * (c1 - c0) + c - c0
                            nc.tensor.matmul_mx(
                                out=bank[:, at : at + U], lhsT=lhs, lhsT_scale=lhs_s, rhs=rhs, rhs_scale=rhs_s,
                                start=True, stop=True,
                            )
            else:
                for g, b, halves, c0, c1 in items:
                    k0 = 2 * g + halves[0]
                    k1 = 2 * g + halves[-1] + 1
                    i = [j for j, e in enumerate(STORES) if e[0] <= k0 and k1 <= e[1] and e[2] <= c0 and c1 <= e[3]][0]
                    s0, s1, t0, t1, q = STORES[i]
                    width = c1 - c0
                    nc.scalar.activation(
                        out=res[i][:, k0 - s0 : k1 - s0, c0 - t0 : c1 - t0],
                        in_=banks[g][b][:, 0 : len(halves) * width].rearrange("p (h c) -> p h c", c=width),
                        func=TANH,
                    )
                    left[i] -= len(halves) * width
                    if left[i] == 0:
                        queue[q].dma_start(out=dst[:, s0:s1, t0:t1], in_=res[i][:])
